import numpy as np
import ml_dtypes


def mxq(x, axis, fmt="e4m3"):
    dtype, down = {"e4m3": (ml_dtypes.float8_e4m3fn, 7), "e5m2": (ml_dtypes.float8_e5m2, 14)}[fmt]
    v = np.moveaxis(np.asarray(x, np.float32).astype(ml_dtypes.bfloat16).astype(np.float64), axis, -1)
    blocks = v.reshape(v.shape[:-1] + (-1, 32))
    amax = np.abs(blocks).max(-1, keepdims=True)
    byte = np.maximum(np.where(amax > 0, np.frexp(amax)[1] - 1 + 127, 0) - down, 1)
    scale = np.exp2(byte - 127.0)
    codes = (blocks / scale).astype(np.float32).astype(dtype).astype(np.float64)
    return np.moveaxis((codes * scale).reshape(v.shape), -1, axis)


WIDE = False


def mx_kscale(k):
    if not WIDE:
        return np.ones(k)
    levels = np.array([10, -10, 5, -5, 0])
    if k % 512:
        return np.exp2(np.random.permutation(np.resize(levels, k // 32))).repeat(32)
    a = np.empty((k // 512, 16))
    for p in range(k // 512):
        a[p, :8] = np.random.permutation(np.resize(levels, 8))
        for g in range(8):
            far = levels[np.abs(levels - a[p, g]) >= 10]
            a[p, g + 8] = far[np.random.randint(len(far))]
    return np.exp2(a.ravel()).repeat(32)


def f64(x):
    return np.asarray(x).astype(np.float64)


def striped(idx):
    return np.tile(idx.reshape(-1, 16).T, (8, 1)).astype(np.uint16)


def unstriped(offs):
    return offs[:16].T.reshape(-1).astype(np.int64)


def striped8(idx):
    return np.concatenate([x.reshape(-1, 16).T for x in idx]).astype(np.uint16)


def runs(offs, k):
    lists = np.stack([offs[16 * r : 16 * r + 16].T.reshape(-1) for r in range(8)]).astype(np.int64)
    return lists[np.arange(k) % 512 // 64]


def pack_weight(w):
    k, n = w.shape
    w = f64(np.asarray(w, np.float32).astype(ml_dtypes.bfloat16)).reshape(k // 32, 32, n)
    amax = np.abs(w).max(1)
    byte = np.clip(np.where(amax > 0, np.frexp(amax)[1] - 1 + 127 - 7, 1), 1, 254)
    scaled = (w * np.exp2(127.0 - byte)[:, None, :]).reshape(k, n).astype(np.float32)
    words = np.ascontiguousarray(scaled.reshape(k // 512, 128, 4, n).transpose(0, 1, 3, 2)).astype(ml_dtypes.float8_e4m3fn).view(np.uint8)
    return words, np.ascontiguousarray(byte.astype(np.uint8).reshape(k // 512, 16, n))


def unpack_weight(words, scales):
    g, p, n, _ = words.shape
    vals = np.ascontiguousarray(words).view(ml_dtypes.float8_e4m3fn).astype(np.float64) * np.repeat(np.exp2(scales.astype(np.float64) - 127.0), 8, axis=1)[..., None]
    return vals.transpose(0, 1, 3, 2).reshape(g * 512, n)


def sigmoid(v):
    return 1.0 / (1.0 + np.exp(-np.maximum(v, -700.0)))


K, T, S, N, G, H = 512, 2048, 512, 512, 2048, 512


def setup_inputs():
    n = np.random.standard_normal
    s = mx_kscale(K)[:, None]
    u = mx_kscale(S)
    packed_xT = pack_weight(n((K, T)) * s)
    packed_dT = pack_weight(n((K, G)) / s)
    return {
        "x_words": packed_xT[0],
        "x_scales": packed_xT[1],
        "d_words": packed_dT[0],
        "d_scales": packed_dT[1],
        "gn": (np.random.uniform(0.5, 1.5, (H, 1)) * u[:, None]).astype(np.float32),
        "w1": (n((H, N)) / np.sqrt(2 * H) / u[:, None]).astype(np.float32),
        "w2": (n((K, N)) / np.sqrt(2 * K) / s).astype(np.float32),
        "offs": striped(np.random.permutation(T)[:S]),
        "k1": striped8(np.random.randint(0, G, (8, H))),
        "n1": striped(np.random.permutation(S)),
        "n2": striped(np.random.permutation(S)),
        "two": striped(np.random.permutation(T)[:S]),
        "n3": striped(np.random.permutation(S)),
        "n4": striped(np.random.permutation(S)),
    }


def reference(x_words, x_scales, d_words, d_scales, gn, w1, w2, offs, k1, n1, n2, two, n3, n4):
    d_k1 = unpack_weight(d_words, d_scales)[np.arange(K)[:, None], runs(k1, K)]
    xq = unpack_weight(x_words, x_scales)[:, unstriped(offs)]
    s = 0.0625 * (d_k1.T @ xq)
    z = f64(gn) * ((s - s[:, unstriped(n1)]) * (sigmoid(s[:, unstriped(n2)])))
    x_two = unpack_weight(x_words, x_scales)[:, unstriped(two)]
    h = mxq(f64(w1), 0, "e4m3").T @ mxq(z, 0, "e4m3") + mxq(f64(w2), 0, "e4m3").T @ x_two
    ex = np.exp(0.5 * h)
    return (2.0 * ex) / (ex + ex[:, unstriped(n3)] + ex[:, unstriped(n4)])

@@ -1,0 +1,223 @@
+from contextlib import ExitStack
+
+import concourse.mybir as mybir
+from concourse.masks import make_identity
+
+K, T, S, N, G, H = 512, 2048, 512, 512, 2048, 512
+FLOPS = 2 * K * H * S + 2 * H * N * S + 2 * K * N * S
+
+F32 = mybir.dt.float32
+BF16 = mybir.dt.bfloat16
+I32 = mybir.dt.int32
+U32 = mybir.dt.uint32
+U16 = mybir.dt.uint16
+U8 = mybir.dt.uint8
+FP8X4 = mybir.dt.float8_e4m3fn_x4
+ACT = mybir.ActivationFunctionType
+ALU = mybir.AluOpType
+
+P = 128
+PACK = 4
+HALF = S // 2
+LIST_COLS = HALF // 16
+
+
+def tile_picked_kmixgdifshare_none_p_kernel(
+    tc, x_words, x_scales, d_words, d_scales, gn, w1, w2, offs, k1, n1, n2, two, n3, n4, out
+):
+    nc = tc.nc
+    with ExitStack() as ctx:
+        sb = ctx.enter_context(tc.tile_pool(name="sb", bufs=1))
+        ps = ctx.enter_context(tc.psum_pool(name="ps", bufs=1))
+
+        def tile(name, shape, dtype):
+            return sb.tile(shape, dtype, name=name, align_bytes=64)
+
+        def load_list(name, src):
+            lst = sb.tile([P, S // 16], U16, name=name)
+            nc.sync.dma_start(lst[:], src)
+            return lst
+
+        def half_of(lst, h):
+            return lst[:, h * LIST_COLS : (h + 1) * LIST_COLS]
+
+        d_scale_win = tile("d_scale_win", [P, G], U8)
+        x_scale_win = tile("x_scale_win", [P, T], U8)
+        nc.vector.memset(d_scale_win[:].bitcast(I32), 0)
+        nc.vector.memset(x_scale_win[:].bitcast(I32), 0)
+
+        k1_l = load_list("k1_l", k1)
+        offs_l = load_list("offs_l", offs)
+        nc.sync.dma_start(out=d_scale_win[0:P:8, :].bitcast(I32), in_=d_scales[0].bitcast(I32))
+        d_word_win = tile("d_word_win", [P, G], I32)
+        nc.sync.dma_start(out=d_word_win[:], in_=d_words[0].rearrange("p c r -> p (c r)").bitcast(I32))
+        for q in range(4):
+            nc.sync.dma_start(
+                out=x_scale_win[32 * q : 32 * q + 4, :].bitcast(I32),
+                in_=x_scales[0][4 * q : 4 * q + 4, :].bitcast(I32),
+            )
+        x_word_win = tile("x_word_win", [P, T], I32)
+        nc.sync.dma_start(out=x_word_win[:], in_=x_words[0].rearrange("p c r -> p (c r)").bitcast(I32))
+        n1_l = load_list("n1_l", n1)
+        n2_l = load_list("n2_l", n2)
+        gn_sb = tile("gn_sb", [P, PACK], F32)
+        nc.sync.dma_start(out=gn_sb[:], in_=gn.rearrange("(p t) o -> p (t o)", t=PACK))
+        w1_raw = tile("w1_raw", [P, PACK, N], F32)
+        nc.sync.dma_start(out=w1_raw[:], in_=w1.rearrange("(p t) m -> p t m", t=PACK))
+        two_l = load_list("two_l", two)
+        w2_raw = tile("w2_raw", [P, PACK, N], F32)
+        nc.sync.dma_start(out=w2_raw[:], in_=w2.rearrange("(p t) m -> p t m", t=PACK))
+        n3_l = load_list("n3_l", n3)
+        n4_l = load_list("n4_l", n4)
+        ident = tile("ident", [P, P], F32)
+        make_identity(nc, ident[:])
+
+        key_bytes = tile("key_bytes", [P, H], U8)
+        nc.vector.tensor_copy(out=key_bytes[:], in_=d_scale_win[:].indirect(k1_l[:]))
+        key_bytes_dealt = tile("key_bytes_dealt", [P, H], U8)
+        nc.vector.tensor_copy(
+            out=key_bytes_dealt[:].rearrange("p (t c i) -> p c t i", t=PACK, i=16),
+            in_=key_bytes[:].rearrange("p (c i t) -> p c t i", t=PACK, i=16),
+        )
+        key_scales = tile("key_scales", [P, H], U8)
+        nc.vector.tensor_copy(out=key_scales[:].bitcast(I32), in_=key_bytes_dealt[:].bitcast(I32))
+        for r in range(1, 4):
+            nc.scalar.dma_start(
+                out=key_scales[r:P:32, :].bitcast(I32),
+                in_=key_bytes_dealt[8 * r : P : 32, :].bitcast(I32),
+            )
+        xq_scales = tile("xq_scales", [P, S], U8)
+        nc.vector.tensor_copy(out=xq_scales[:], in_=x_scale_win[:].indirect(offs_l[:]))
+        key_words = tile("key_words", [P, H], U32)
+        nc.vector.tensor_copy(out=key_words[:], in_=d_word_win[:].bitcast(U32).indirect(k1_l[:]))
+        key_codes = tile("key_codes", [P, H], U32)
+        nc.vector.tensor_copy(
+            out=key_codes[:].rearrange("p (t c i) -> p c t i", t=PACK, i=4),
+            in_=key_words[:].rearrange("p (c i t) -> p c t i", t=PACK, i=4),
+        )
+        xq_codes = tile("xq_codes", [P, S], U32)
+        nc.vector.tensor_copy(out=xq_codes[:], in_=x_word_win[:].bitcast(U32).indirect(offs_l[:]))
+
+        s_rows = [tile(f"s_rows{t}", [P, S], F32) for t in range(PACK)]
+
+        def score(t):
+            bank = ps.tile([P, S], F32, name=f"s_bank{t}", tag="lo3")
+            cols = slice(t * P, (t + 1) * P)
+            nc.tensor.matmul_mx(
+                out=bank[:],
+                lhsT=key_codes[:, cols].bitcast(FP8X4),
+                lhsT_scale=key_scales[:, cols],
+                rhs=xq_codes[:].bitcast(FP8X4),
+                rhs_scale=xq_scales[:],
+                start=True,
+                stop=True,
+            )
+            if t == 0:
+                nc.vector.tensor_scalar_mul(out=s_rows[t][:], in0=bank[:], scalar1=0.0625)
+            else:
+                nc.scalar.activation(out=s_rows[t][:], in_=bank[:], func=ACT.Copy, scale=0.0625)
+
+        score(0)
+        x2_codes = tile("x2_codes", [P, S], U32)
+        nc.vector.tensor_copy(out=x2_codes[:], in_=x_word_win[:].bitcast(U32).indirect(two_l[:]))
+        x2_scales = tile("x2_scales", [P, S], U8)
+        nc.vector.tensor_copy(out=x2_scales[:], in_=x_scale_win[:].indirect(two_l[:]))
+
+        def interleave(name, planes, width):
+            grouped = tile(name, [P, width * PACK], BF16)
+            nc.vector.tensor_copy(
+                out=grouped[:].rearrange("p (c i t) -> p c t i", t=PACK, i=4),
+                in_=planes[:].rearrange("p t (c i) -> p c t i", i=4),
+            )
+            return grouped
+
+        def quantize(name, grouped, width):
+            codes = tile(name + "_codes", [P, width], U32)
+            scales = tile(name + "_scales", [P, width], U8)
+            nc.vector.quantize_mx(out=codes[:].bitcast(FP8X4), scales=scales[:], in_=grouped[:])
+            return codes, scales
+
+        w1_grouped = interleave("w1_grouped", w1_raw, N)
+        w2_grouped = interleave("w2_grouped", w2_raw, N)
+        w1_codes, w1_scales = quantize("w1", w1_grouped, N)
+        w2_codes, w2_scales = quantize("w2", w2_grouped, N)
+
+        ex = [tile(f"ex{m}", [P, S], F32) for m in range(PACK)]
+        h_banks = {}
+        for h in range(2):
+            cols = slice(h * HALF, (h + 1) * HALF)
+            z_planes = tile(f"z_planes{h}", [P, PACK, HALF], BF16)
+            for t in range(PACK):
+                if h == 0 and t > 0:
+                    score(t)
+                gate = tile(f"gate{h}{t}", [P, HALF], F32)
+                nc.scalar.activation(out=gate[:], in_=s_rows[t][:].indirect(half_of(n2_l, h)), func=ACT.Sigmoid)
+                s_n1 = tile(f"s_n1_{h}{t}", [P, HALF], F32)
+                nc.scalar.activation(out=s_n1[:], in_=s_rows[t][:].indirect(half_of(n1_l, h)), func=ACT.Copy)
+                diff = tile(f"diff{h}{t}", [P, HALF], F32)
+                nc.vector.tensor_tensor(out=diff[:], in0=s_rows[t][:, cols], in1=s_n1[:], op=ALU.subtract)
+                nc.vector.scalar_tensor_tensor(
+                    out=z_planes[:, t, :], in0=diff[:], scalar=gn_sb[:, t : t + 1], in1=gate[:],
+                    op0=ALU.mult, op1=ALU.mult,
+                )
+            z_grouped = interleave(f"z_grouped{h}", z_planes, HALF)
+            z_codes, z_scales = quantize(f"z{h}", z_grouped, HALF)
+            for m in range(PACK):
+                rows = slice(m * P, (m + 1) * P)
+                bank = ps.tile([P, HALF], F32, name=f"h_bank{h}{m}", tag=f"hi{m}" if h == 0 else f"lo{m}")
+                nc.tensor.matmul_mx(
+                    out=bank[:],
+                    lhsT=w2_codes[:, rows].bitcast(FP8X4),
+                    lhsT_scale=w2_scales[:, rows],
+                    rhs=x2_codes[:, cols].bitcast(FP8X4),
+                    rhs_scale=x2_scales[:, cols],
+                    start=True,
+                    stop=False,
+                )
+                nc.tensor.matmul_mx(
+                    out=bank[:],
+                    lhsT=w1_codes[:, rows].bitcast(FP8X4),
+                    lhsT_scale=w1_scales[:, rows],
+                    rhs=z_codes[:].bitcast(FP8X4),
+                    rhs_scale=z_scales[:],
+                    start=False,
+                    stop=True,
+                )
+                h_banks[h, m] = bank
+
+        for h in range(2):
+            for m in range(PACK):
+                nc.scalar.activation(
+                    out=ex[m][:, h * HALF : (h + 1) * HALF], in_=h_banks[h, m][:], func=ACT.Exp, scale=0.5
+                )
+
+        for m in range(PACK):
+            for h in range(2):
+                cols = slice(h * HALF, (h + 1) * HALF)
+                ex_n3 = tile(f"ex_n3_{m}{h}", [P, HALF], F32)
+                nc.scalar.activation(out=ex_n3[:], in_=ex[m][:].indirect(half_of(n3_l, h)), func=ACT.Copy)
+                ex_n4 = tile(f"ex_n4_{m}{h}", [P, HALF], F32)
+                nc.vector.tensor_copy(out=ex_n4[:], in_=ex[m][:].indirect(half_of(n4_l, h)))
+                unit = 2 * m + h
+                den_t = ps.tile([P, HALF], F32, name=f"den_t{m}{h}", tag=f"hi{unit % PACK}")
+                for c in range(HALF // P):
+                    chunk = slice(c * P, (c + 1) * P)
+                    terms = (ex[m][:, h * HALF + c * P : h * HALF + (c + 1) * P], ex_n4[:, chunk], ex_n3[:, chunk])
+                    for i, term in enumerate(terms):
+                        nc.tensor.matmul(
+                            out=den_t[:, chunk], lhsT=term, rhs=ident[:], is_transpose=True,
+                            start=(i == 0), stop=(i == len(terms) - 1),
+                        )
+                root_t = tile(f"root_t{m}{h}", [P, HALF], F32)
+                nc.scalar.activation(out=root_t[:], in_=den_t[:], func=ACT.Abs_reciprocal_sqrt)
+                root = ps.tile([P, HALF], F32, name=f"root{m}{h}", tag=f"lo{unit % PACK}")
+                for c in range(HALF // P):
+                    chunk = slice(c * P, (c + 1) * P)
+                    nc.tensor.transpose(out=root[:, chunk], in_=root_t[:, chunk], identity=ident[:])
+                part = tile(f"part{m}{h}", [P, HALF], F32)
+                nc.vector.scalar_tensor_tensor(
+                    out=part[:], in0=ex[m][:, cols], scalar=2.0, in1=root[:], op0=ALU.mult, op1=ALU.mult
+                )
+                res = tile(f"res{m}{h}", [P, HALF], F32)
+                nc.vector.tensor_tensor(out=res[:], in0=part[:], in1=root[:], op=ALU.mult)
+                nc.sync.dma_start(out=out[m * P : (m + 1) * P, cols], in_=res[:])

@@ -19,7 +19,12 @@ ALU = mybir.AluOpType
 P = 128
 PACK = 4
 HALF = S // 2
-LIST_COLS = HALF // 16
+SPARE = 32
+EARLY_TILES = 4
+WEIGHT_PARTS = (slice(0, EARLY_TILES * P), slice(EARLY_TILES * P, N))
+S_TILES_COPIED_BY_VECTOR = (2, 3)
+PIECES = ((0, 0, 512), (1, 0, 512), (2, 0, 512), (3, 0, 256), (3, 256, 128), (3, 384, 128))
+SQUARED_ON_SCALAR = ()
 
 
 def tile_picked_kmixgdifshare_none_p_kernel(
@@ -30,16 +35,19 @@ def tile_picked_kmixgdifshare_none_p_kernel(
         sb = ctx.enter_context(tc.tile_pool(name="sb", bufs=1))
         ps = ctx.enter_context(tc.psum_pool(name="ps", bufs=1))
 
-        def tile(name, shape, dtype):
-            return sb.tile(shape, dtype, name=name, align_bytes=64)
+        def tile(name, shape, dtype, tag=None):
+            return sb.tile(shape, dtype, name=name, tag=tag or name, align_bytes=64)
+
+        def bank(name, width, number):
+            return ps.tile([P, width], F32, name=name, tag=f"bank{number}")
 
         def load_list(name, src):
             lst = sb.tile([P, S // 16], U16, name=name)
             nc.sync.dma_start(lst[:], src)
             return lst
 
-        def half_of(lst, h):
-            return lst[:, h * LIST_COLS : (h + 1) * LIST_COLS]
+        def entries(lst, first, count):
+            return lst[:, first // 16 : (first + count) // 16]
 
         d_scale_win = tile("d_scale_win", [P, G], U8)
         x_scale_win = tile("x_scale_win", [P, T], U8)
@@ -56,21 +64,20 @@ def tile_picked_kmixgdifshare_none_p_kernel(
                 out=x_scale_win[32 * q : 32 * q + 4, :].bitcast(I32),
                 in_=x_scales[0][4 * q : 4 * q + 4, :].bitcast(I32),
             )
-        x_word_win = tile("x_word_win", [P, T], I32)
-        nc.sync.dma_start(out=x_word_win[:], in_=x_words[0].rearrange("p c r -> p (c r)").bitcast(I32))
         n1_l = load_list("n1_l", n1)
         n2_l = load_list("n2_l", n2)
-        gn_sb = tile("gn_sb", [P, PACK], F32)
-        nc.sync.dma_start(out=gn_sb[:], in_=gn.rearrange("(p t) o -> p (t o)", t=PACK))
-        w1_raw = tile("w1_raw", [P, PACK, N], F32)
-        nc.sync.dma_start(out=w1_raw[:], in_=w1.rearrange("(p t) m -> p t m", t=PACK))
+        x_word_win = tile("x_word_win", [P, T], I32)
+        nc.sync.dma_start(out=x_word_win[:], in_=x_words[0].rearrange("p c r -> p (c r)").bitcast(I32))
         two_l = load_list("two_l", two)
-        w2_raw = tile("w2_raw", [P, PACK, N], F32)
-        nc.sync.dma_start(out=w2_raw[:], in_=w2.rearrange("(p t) m -> p t m", t=PACK))
         n3_l = load_list("n3_l", n3)
         n4_l = load_list("n4_l", n4)
+        gn_sb = tile("gn_sb", [P, PACK], F32)
+        nc.gpsimd.dma_start(out=gn_sb[:], in_=gn.rearrange("(p t) o -> p (t o)", t=PACK))
         ident = tile("ident", [P, P], F32)
         make_identity(nc, ident[:])
+        ex = [tile(f"ex{m}", [P, S + SPARE], F32) for m in range(PACK)]
+        for m in range(PACK):
+            nc.gpsimd.memset(ex[m][:, S:], 0.0)
 
         key_bytes = tile("key_bytes", [P, H], U8)
         nc.vector.tensor_copy(out=key_bytes[:], in_=d_scale_win[:].indirect(k1_l[:]))
@@ -95,129 +102,163 @@ def tile_picked_kmixgdifshare_none_p_kernel(
             out=key_codes[:].rearrange("p (t c i) -> p c t i", t=PACK, i=4),
             in_=key_words[:].rearrange("p (c i t) -> p c t i", t=PACK, i=4),
         )
+
+        def load_weight(name, w, part, tag):
+            cols = WEIGHT_PARTS[part]
+            raw = tile(name, [P, PACK, cols.stop - cols.start], F32, tag=tag)
+            nc.sync.dma_start(out=raw[:], in_=w[:, cols].rearrange("(p t) m -> p t m", t=PACK))
+            return raw
+
+        w_raw = {}
+        w_raw[1, 0] = load_weight("w1_raw0", w1, 0, "d_word_win")
+        w_raw[2, 0] = load_weight("w2_raw0", w2, 0, "key_words")
         xq_codes = tile("xq_codes", [P, S], U32)
         nc.vector.tensor_copy(out=xq_codes[:], in_=x_word_win[:].bitcast(U32).indirect(offs_l[:]))
 
-        s_rows = [tile(f"s_rows{t}", [P, S], F32) for t in range(PACK)]
-
-        def score(t):
-            bank = ps.tile([P, S], F32, name=f"s_bank{t}", tag="lo3")
-            cols = slice(t * P, (t + 1) * P)
+        s_banks = [bank(f"s_bank{t}", S, t) for t in range(PACK)]
+        for t in range(PACK):
+            keys = slice(t * P, (t + 1) * P)
             nc.tensor.matmul_mx(
-                out=bank[:],
-                lhsT=key_codes[:, cols].bitcast(FP8X4),
-                lhsT_scale=key_scales[:, cols],
+                out=s_banks[t][:],
+                lhsT=key_codes[:, keys].bitcast(FP8X4),
+                lhsT_scale=key_scales[:, keys],
                 rhs=xq_codes[:].bitcast(FP8X4),
                 rhs_scale=xq_scales[:],
                 start=True,
                 stop=True,
             )
-            if t == 0:
-                nc.vector.tensor_scalar_mul(out=s_rows[t][:], in0=bank[:], scalar1=0.0625)
-            else:
-                nc.scalar.activation(out=s_rows[t][:], in_=bank[:], func=ACT.Copy, scale=0.0625)
+        s_rows = [tile(f"s_rows{t}", [P, S], F32) for t in range(PACK)]
+        for t in S_TILES_COPIED_BY_VECTOR:
+            nc.vector.tensor_scalar_mul(out=s_rows[t][:], in0=s_banks[t][:], scalar1=0.0625)
 
-        score(0)
         x2_codes = tile("x2_codes", [P, S], U32)
         nc.vector.tensor_copy(out=x2_codes[:], in_=x_word_win[:].bitcast(U32).indirect(two_l[:]))
         x2_scales = tile("x2_scales", [P, S], U8)
         nc.vector.tensor_copy(out=x2_scales[:], in_=x_scale_win[:].indirect(two_l[:]))
 
-        def interleave(name, planes, width):
-            grouped = tile(name, [P, width * PACK], BF16)
+        def interleave(name, planes):
+            grouped = tile(name, [P, planes.shape[2] * PACK], BF16)
             nc.vector.tensor_copy(
                 out=grouped[:].rearrange("p (c i t) -> p c t i", t=PACK, i=4),
                 in_=planes[:].rearrange("p t (c i) -> p c t i", i=4),
             )
             return grouped
 
-        def quantize(name, grouped, width):
-            codes = tile(name + "_codes", [P, width], U32)
-            scales = tile(name + "_scales", [P, width], U8)
-            nc.vector.quantize_mx(out=codes[:].bitcast(FP8X4), scales=scales[:], in_=grouped[:])
-            return codes, scales
+        def quantize_weights(part):
+            grouped = {n: interleave(f"w{n}_grouped{part}", w_raw[n, part]) for n in (1, 2)}
+            width = WEIGHT_PARTS[part].stop - WEIGHT_PARTS[part].start
+            made = {}
+            for n in (1, 2):
+                codes = tile(f"w{n}_codes{part}", [P, width], U32)
+                scales = tile(f"w{n}_scales{part}", [P, width], U8)
+                nc.vector.quantize_mx(out=codes[:].bitcast(FP8X4), scales=scales[:], in_=grouped[n][:])
+                made[n] = (codes, scales)
+            return made
 
-        w1_grouped = interleave("w1_grouped", w1_raw, N)
-        w2_grouped = interleave("w2_grouped", w2_raw, N)
-        w1_codes, w1_scales = quantize("w1", w1_grouped, N)
-        w2_codes, w2_scales = quantize("w2", w2_grouped, N)
+        z_codes = tile("z_codes", [P, S], U32)
+        z_scales = tile("z_scales", [P, S], U8)
 
-        ex = [tile(f"ex{m}", [P, S], F32) for m in range(PACK)]
-        h_banks = {}
+        def exp_half_h(m, cols, weights, number):
+            rows = slice(m % EARLY_TILES * P, (m % EARLY_TILES + 1) * P)
+            h_bank = bank(f"h_bank{m}_{cols.start}", cols.stop - cols.start, number)
+            moving = {2: (x2_codes, x2_scales), 1: (z_codes, z_scales)}
+            for n in (2, 1):
+                nc.tensor.matmul_mx(
+                    out=h_bank[:],
+                    lhsT=weights[n][0][:, rows].bitcast(FP8X4),
+                    lhsT_scale=weights[n][1][:, rows],
+                    rhs=moving[n][0][:, cols].bitcast(FP8X4),
+                    rhs_scale=moving[n][1][:, cols],
+                    start=(n == 2),
+                    stop=(n == 1),
+                )
+            return lambda: nc.scalar.activation(out=ex[m][:, cols], in_=h_bank[:], func=ACT.Exp, scale=0.5)
+
+        early_weights = quantize_weights(0)
+        exps = []
         for h in range(2):
             cols = slice(h * HALF, (h + 1) * HALF)
             z_planes = tile(f"z_planes{h}", [P, PACK, HALF], BF16)
             for t in range(PACK):
-                if h == 0 and t > 0:
-                    score(t)
-                gate = tile(f"gate{h}{t}", [P, HALF], F32)
-                nc.scalar.activation(out=gate[:], in_=s_rows[t][:].indirect(half_of(n2_l, h)), func=ACT.Sigmoid)
+                if h == 0 and t not in S_TILES_COPIED_BY_VECTOR:
+                    nc.scalar.activation(out=s_rows[t][:], in_=s_banks[t][:], func=ACT.Copy, scale=0.0625)
                 s_n1 = tile(f"s_n1_{h}{t}", [P, HALF], F32)
-                nc.scalar.activation(out=s_n1[:], in_=s_rows[t][:].indirect(half_of(n1_l, h)), func=ACT.Copy)
+                nc.scalar.activation(
+                    out=s_n1[:], in_=s_rows[t][:].indirect(entries(n1_l, cols.start, HALF)), func=ACT.Copy
+                )
+                gate = tile(f"gate{h}{t}", [P, HALF], F32)
+                nc.scalar.activation(
+                    out=gate[:], in_=s_rows[t][:].indirect(entries(n2_l, cols.start, HALF)), func=ACT.Sigmoid
+                )
                 diff = tile(f"diff{h}{t}", [P, HALF], F32)
                 nc.vector.tensor_tensor(out=diff[:], in0=s_rows[t][:, cols], in1=s_n1[:], op=ALU.subtract)
                 nc.vector.scalar_tensor_tensor(
                     out=z_planes[:, t, :], in0=diff[:], scalar=gn_sb[:, t : t + 1], in1=gate[:],
                     op0=ALU.mult, op1=ALU.mult,
                 )
-            z_grouped = interleave(f"z_grouped{h}", z_planes, HALF)
-            z_codes, z_scales = quantize(f"z{h}", z_grouped, HALF)
-            for m in range(PACK):
-                rows = slice(m * P, (m + 1) * P)
-                bank = ps.tile([P, HALF], F32, name=f"h_bank{h}{m}", tag=f"hi{m}" if h == 0 else f"lo{m}")
-                nc.tensor.matmul_mx(
-                    out=bank[:],
-                    lhsT=w2_codes[:, rows].bitcast(FP8X4),
-                    lhsT_scale=w2_scales[:, rows],
-                    rhs=x2_codes[:, cols].bitcast(FP8X4),
-                    rhs_scale=x2_scales[:, cols],
-                    start=True,
-                    stop=False,
-                )
-                nc.tensor.matmul_mx(
-                    out=bank[:],
-                    lhsT=w1_codes[:, rows].bitcast(FP8X4),
-                    lhsT_scale=w1_scales[:, rows],
-                    rhs=z_codes[:].bitcast(FP8X4),
-                    rhs_scale=z_scales[:],
-                    start=False,
-                    stop=True,
-                )
-                h_banks[h, m] = bank
+            z_grouped = interleave(f"z_grouped{h}", z_planes)
+            nc.vector.quantize_mx(out=z_codes[:, cols].bitcast(FP8X4), scales=z_scales[:, cols], in_=z_grouped[:])
+            for m in range(EARLY_TILES):
+                exps.append(exp_half_h(m, cols, early_weights, (4 + EARLY_TILES * h + m) % 8))
 
-        for h in range(2):
-            for m in range(PACK):
-                nc.scalar.activation(
-                    out=ex[m][:, h * HALF : (h + 1) * HALF], in_=h_banks[h, m][:], func=ACT.Exp, scale=0.5
+        for run in exps:
+            run()
+
+        ex_n3, ex_n4 = {}, {}
+
+        def fetch_n3(u):
+            m, first, width = PIECES[u]
+            ex_n3[u] = tile(f"ex_n3_{u}", [P, width], F32, tag=f"ex_n3_{u % 2}")
+            nc.scalar.activation(out=ex_n3[u][:], in_=ex[m][:].indirect(entries(n3_l, first, width)), func=ACT.Copy)
+
+        def fetch_n4(u):
+            m, first, width = PIECES[u]
+            ex_n4[u] = tile(f"ex_n4_{u}", [P, width], F32)
+            for c in range(0, width, HALF):
+                count = min(HALF, width - c)
+                nc.vector.tensor_copy(
+                    out=ex_n4[u][:, c : c + count], in_=ex[m][:].indirect(entries(n4_l, first + c, count))
                 )
 
-        for m in range(PACK):
-            for h in range(2):
-                cols = slice(h * HALF, (h + 1) * HALF)
-                ex_n3 = tile(f"ex_n3_{m}{h}", [P, HALF], F32)
-                nc.scalar.activation(out=ex_n3[:], in_=ex[m][:].indirect(half_of(n3_l, h)), func=ACT.Copy)
-                ex_n4 = tile(f"ex_n4_{m}{h}", [P, HALF], F32)
-                nc.vector.tensor_copy(out=ex_n4[:], in_=ex[m][:].indirect(half_of(n4_l, h)))
-                unit = 2 * m + h
-                den_t = ps.tile([P, HALF], F32, name=f"den_t{m}{h}", tag=f"hi{unit % PACK}")
-                for c in range(HALF // P):
-                    chunk = slice(c * P, (c + 1) * P)
-                    terms = (ex[m][:, h * HALF + c * P : h * HALF + (c + 1) * P], ex_n4[:, chunk], ex_n3[:, chunk])
-                    for i, term in enumerate(terms):
-                        nc.tensor.matmul(
-                            out=den_t[:, chunk], lhsT=term, rhs=ident[:], is_transpose=True,
-                            start=(i == 0), stop=(i == len(terms) - 1),
-                        )
-                root_t = tile(f"root_t{m}{h}", [P, HALF], F32)
-                nc.scalar.activation(out=root_t[:], in_=den_t[:], func=ACT.Abs_reciprocal_sqrt)
-                root = ps.tile([P, HALF], F32, name=f"root{m}{h}", tag=f"lo{unit % PACK}")
-                for c in range(HALF // P):
-                    chunk = slice(c * P, (c + 1) * P)
-                    nc.tensor.transpose(out=root[:, chunk], in_=root_t[:, chunk], identity=ident[:])
-                part = tile(f"part{m}{h}", [P, HALF], F32)
-                nc.vector.scalar_tensor_tensor(
-                    out=part[:], in0=ex[m][:, cols], scalar=2.0, in1=root[:], op0=ALU.mult, op1=ALU.mult
-                )
-                res = tile(f"res{m}{h}", [P, HALF], F32)
+        def finish(u):
+            m, first, width = PIECES[u]
+            cols = slice(first, first + width)
+            den_t = bank(f"den_t{u}", width, 4 + u % 4)
+            terms = (ex_n4[u][:], ex[m][:, cols], ex_n3[u][:])
+            for i, term in enumerate(terms):
+                for c in range(0, width, P):
+                    nc.tensor.matmul(
+                        out=den_t[:, c : c + P], lhsT=term[:, c : c + P], rhs=ident[:], is_transpose=True,
+                        start=(i == 0 and c == 0), stop=(i == len(terms) - 1 and c + P == width),
+                    )
+            root_t = tile(f"root_t{u}", [P, width], F32)
+            nc.scalar.activation(out=root_t[:], in_=den_t[:], func=ACT.Abs_reciprocal_sqrt)
+            if u in SQUARED_ON_SCALAR:
+                inv_t = tile(f"inv_t{u}", [P, width], F32)
+                nc.scalar.activation(out=inv_t[:], in_=root_t[:], func=ACT.Square)
+                root_t = inv_t
+            root = bank(f"root{u}", width, u % 4)
+            for c in range(0, width, P):
+                nc.tensor.transpose(out=root[:, c : c + P], in_=root_t[:, c : c + P], identity=ident[:])
+            part = tile(f"part{u}", [P, width], F32)
+            nc.vector.scalar_tensor_tensor(
+                out=part[:], in0=ex[m][:, cols], scalar=2.0, in1=root[:], op0=ALU.mult, op1=ALU.mult
+            )
+            res = part
+            if u not in SQUARED_ON_SCALAR:
+                res = tile(f"res{u}", [P, width], F32)
                 nc.vector.tensor_tensor(out=res[:], in0=part[:], in1=root[:], op=ALU.mult)
-                nc.sync.dma_start(out=out[m * P : (m + 1) * P, cols], in_=res[:])
+            nc.sync.dma_start(out=out[m * P : (m + 1) * P, cols], in_=res[:])
+
+        for u in range(2):
+            fetch_n3(u)
+        for u in range(2, 2):
+            fetch_n3(u)
+        for u in range(2):
+            fetch_n4(u)
+        for u in range(len(PIECES)):
+            finish(u)
+            if u + 2 < len(PIECES):
+                fetch_n3(u + 2)
+            if u + 2 < len(PIECES):
+                fetch_n4(u + 2)

@@ -54,6 +54,11 @@ def tile_picked_kmixgdifshare_none_p_kernel(
         nc.vector.memset(d_scale_win[:].bitcast(I32), 0)
         nc.vector.memset(x_scale_win[:].bitcast(I32), 0)
 
+        warm_in = tile("warm_in", [P, 1], F32)
+        nc.gpsimd.memset(warm_in[:], 0.0)
+        warm_out = tile("warm_out", [P, 1], F32)
+        nc.scalar.activation(out=warm_out[:], in_=warm_in[:], func=ACT.Sigmoid)
+
         k1_l = load_list("k1_l", k1)
         offs_l = load_list("offs_l", offs)
         nc.sync.dma_start(out=d_scale_win[0:P:8, :].bitcast(I32), in_=d_scales[0].bitcast(I32))

@@ -18,13 +18,15 @@ ALU = mybir.AluOpType
 
 P = 128
 PACK = 4
+LAST = PACK - 1
 HALF = S // 2
+S_SCALE = 0.0625
+LIST_GROUP = 16
+BLOCK_PARTITIONS = 8
+QUADRANT = 32
 SPARE = 32
-EARLY_TILES = 4
-WEIGHT_PARTS = (slice(0, EARLY_TILES * P), slice(EARLY_TILES * P, N))
-S_TILES_COPIED_BY_VECTOR = (2, 3)
-PIECES = ((0, 0, 512), (1, 0, 512), (2, 0, 512), (3, 0, 256), (3, 256, 128), (3, 384, 128))
-SQUARED_ON_SCALAR = ()
+PIECE_WIDTHS = ((S,), (S,), (HALF, HALF), (HALF, P, P))
+PIECES_AHEAD = 2
 
 
 def tile_picked_kmixgdifshare_none_p_kernel(
@@ -42,12 +44,23 @@ def tile_picked_kmixgdifshare_none_p_kernel(
             return ps.tile([P, width], F32, name=name, tag=f"bank{number}")
 
         def load_list(name, src):
-            lst = sb.tile([P, S // 16], U16, name=name)
+            lst = sb.tile([P, S // LIST_GROUP], U16, name=name)
             nc.sync.dma_start(lst[:], src)
             return lst
 
         def entries(lst, first, count):
-            return lst[:, first // 16 : (first + count) // 16]
+            return lst[:, first // LIST_GROUP : (first + count) // LIST_GROUP]
+
+        def mx_pass(acc, stationary, moving, start, stop):
+            nc.tensor.matmul_mx(
+                out=acc,
+                lhsT=stationary[0].bitcast(FP8X4),
+                lhsT_scale=stationary[1],
+                rhs=moving[0].bitcast(FP8X4),
+                rhs_scale=moving[1],
+                start=start,
+                stop=stop,
+            )
 
         d_scale_win = tile("d_scale_win", [P, G], U8)
         x_scale_win = tile("x_scale_win", [P, T], U8)
@@ -61,18 +74,19 @@ def tile_picked_kmixgdifshare_none_p_kernel(
 
         k1_l = load_list("k1_l", k1)
         offs_l = load_list("offs_l", offs)
-        nc.sync.dma_start(out=d_scale_win[0:P:8, :].bitcast(I32), in_=d_scales[0].bitcast(I32))
+        nc.sync.dma_start(out=d_scale_win[0:P:BLOCK_PARTITIONS, :].bitcast(I32), in_=d_scales[0].bitcast(I32))
         d_word_win = tile("d_word_win", [P, G], I32)
         nc.sync.dma_start(out=d_word_win[:], in_=d_words[0].rearrange("p c r -> p (c r)").bitcast(I32))
-        for q in range(4):
-            nc.sync.dma_start(
-                out=x_scale_win[32 * q : 32 * q + 4, :].bitcast(I32),
+        for q in range(P // QUADRANT):
+            queue = nc.sync if q == 0 else nc.scalar
+            queue.dma_start(
+                out=x_scale_win[QUADRANT * q : QUADRANT * q + 4, :].bitcast(I32),
                 in_=x_scales[0][4 * q : 4 * q + 4, :].bitcast(I32),
             )
         n1_l = load_list("n1_l", n1)
-        n2_l = load_list("n2_l", n2)
         x_word_win = tile("x_word_win", [P, T], I32)
         nc.sync.dma_start(out=x_word_win[:], in_=x_words[0].rearrange("p c r -> p (c r)").bitcast(I32))
+        n2_l = load_list("n2_l", n2)
         two_l = load_list("two_l", two)
         n3_l = load_list("n3_l", n3)
         n4_l = load_list("n4_l", n4)
@@ -80,9 +94,12 @@ def tile_picked_kmixgdifshare_none_p_kernel(
         nc.gpsimd.dma_start(out=gn_sb[:], in_=gn.rearrange("(p t) o -> p (t o)", t=PACK))
         ident = tile("ident", [P, P], F32)
         make_identity(nc, ident[:])
-        ex = [tile(f"ex{m}", [P, S + SPARE], F32) for m in range(PACK)]
-        for m in range(PACK):
-            nc.gpsimd.memset(ex[m][:, S:], 0.0)
+        ex = []
+        for m, widths in enumerate(PIECE_WIDTHS):
+            spare = SPARE if S in widths else 0
+            ex.append(tile(f"ex{m}", [P, S + spare], F32))
+            if spare:
+                nc.gpsimd.memset(ex[m][:, S:], 0.0)
 
         key_bytes = tile("key_bytes", [P, H], U8)
         nc.vector.tensor_copy(out=key_bytes[:], in_=d_scale_win[:].indirect(k1_l[:]))
@@ -95,49 +112,35 @@ def tile_picked_kmixgdifshare_none_p_kernel(
         nc.vector.tensor_copy(out=key_scales[:].bitcast(I32), in_=key_bytes_dealt[:].bitcast(I32))
         for r in range(1, 4):
             nc.scalar.dma_start(
-                out=key_scales[r:P:32, :].bitcast(I32),
-                in_=key_bytes_dealt[8 * r : P : 32, :].bitcast(I32),
+                out=key_scales[r:P:QUADRANT, :].bitcast(I32),
+                in_=key_bytes_dealt[BLOCK_PARTITIONS * r : P : QUADRANT, :].bitcast(I32),
             )
         xq_scales = tile("xq_scales", [P, S], U8)
         nc.vector.tensor_copy(out=xq_scales[:], in_=x_scale_win[:].indirect(offs_l[:]))
         key_words = tile("key_words", [P, H], U32)
         nc.vector.tensor_copy(out=key_words[:], in_=d_word_win[:].bitcast(U32).indirect(k1_l[:]))
-        key_codes = tile("key_codes", [P, H], U32)
+        key_words_dealt = tile("key_words_dealt", [P, H], U32)
         nc.vector.tensor_copy(
-            out=key_codes[:].rearrange("p (t c i) -> p c t i", t=PACK, i=4),
+            out=key_words_dealt[:].rearrange("p (t c i) -> p c t i", t=PACK, i=4),
             in_=key_words[:].rearrange("p (c i t) -> p c t i", t=PACK, i=4),
         )
 
-        def load_weight(name, w, part, tag):
-            cols = WEIGHT_PARTS[part]
-            raw = tile(name, [P, PACK, cols.stop - cols.start], F32, tag=tag)
-            nc.sync.dma_start(out=raw[:], in_=w[:, cols].rearrange("(p t) m -> p t m", t=PACK))
-            return raw
-
-        w_raw = {}
-        w_raw[1, 0] = load_weight("w1_raw0", w1, 0, "d_word_win")
-        w_raw[2, 0] = load_weight("w2_raw0", w2, 0, "key_words")
-        xq_codes = tile("xq_codes", [P, S], U32)
-        nc.vector.tensor_copy(out=xq_codes[:], in_=x_word_win[:].bitcast(U32).indirect(offs_l[:]))
+        w1_raw = tile("w1_raw", [P, PACK, N], F32, tag="d_word_win")
+        nc.sync.dma_start(out=w1_raw[:], in_=w1.rearrange("(p t) m -> p t m", t=PACK))
+        w2_raw = tile("w2_raw", [P, PACK, N], F32, tag="key_words")
+        nc.sync.dma_start(out=w2_raw[:], in_=w2.rearrange("(p t) m -> p t m", t=PACK))
+        xq_words = tile("xq_words", [P, S], U32)
+        nc.vector.tensor_copy(out=xq_words[:], in_=x_word_win[:].bitcast(U32).indirect(offs_l[:]))
 
         s_banks = [bank(f"s_bank{t}", S, t) for t in range(PACK)]
         for t in range(PACK):
             keys = slice(t * P, (t + 1) * P)
-            nc.tensor.matmul_mx(
-                out=s_banks[t][:],
-                lhsT=key_codes[:, keys].bitcast(FP8X4),
-                lhsT_scale=key_scales[:, keys],
-                rhs=xq_codes[:].bitcast(FP8X4),
-                rhs_scale=xq_scales[:],
-                start=True,
-                stop=True,
-            )
+            mx_pass(s_banks[t][:], (key_words_dealt[:, keys], key_scales[:, keys]), (xq_words[:], xq_scales[:]), True, True)
         s_rows = [tile(f"s_rows{t}", [P, S], F32) for t in range(PACK)]
-        for t in S_TILES_COPIED_BY_VECTOR:
-            nc.vector.tensor_scalar_mul(out=s_rows[t][:], in0=s_banks[t][:], scalar1=0.0625)
+        nc.vector.tensor_scalar_mul(out=s_rows[LAST][:], in0=s_banks[LAST][:], scalar1=S_SCALE)
 
-        x2_codes = tile("x2_codes", [P, S], U32)
-        nc.vector.tensor_copy(out=x2_codes[:], in_=x_word_win[:].bitcast(U32).indirect(two_l[:]))
+        x2_words = tile("x2_words", [P, S], U32)
+        nc.vector.tensor_copy(out=x2_words[:], in_=x_word_win[:].bitcast(U32).indirect(two_l[:]))
         x2_scales = tile("x2_scales", [P, S], U8)
         nc.vector.tensor_copy(out=x2_scales[:], in_=x_scale_win[:].indirect(two_l[:]))
 
@@ -145,125 +148,121 @@ def tile_picked_kmixgdifshare_none_p_kernel(
             grouped = tile(name, [P, planes.shape[2] * PACK], BF16)
             nc.vector.tensor_copy(
                 out=grouped[:].rearrange("p (c i t) -> p c t i", t=PACK, i=4),
-                in_=planes[:].rearrange("p t (c i) -> p c t i", i=4),
+                in_=planes.rearrange("p t (c i) -> p c t i", i=4),
             )
             return grouped
 
-        def quantize_weights(part):
-            grouped = {n: interleave(f"w{n}_grouped{part}", w_raw[n, part]) for n in (1, 2)}
-            width = WEIGHT_PARTS[part].stop - WEIGHT_PARTS[part].start
-            made = {}
-            for n in (1, 2):
-                codes = tile(f"w{n}_codes{part}", [P, width], U32)
-                scales = tile(f"w{n}_scales{part}", [P, width], U8)
-                nc.vector.quantize_mx(out=codes[:].bitcast(FP8X4), scales=scales[:], in_=grouped[n][:])
-                made[n] = (codes, scales)
-            return made
+        w1_grouped = interleave("w1_grouped", w1_raw[:])
+        w2_grouped = interleave("w2_grouped", w2_raw[:])
+        w1_words = tile("w1_words", [P, N], U32)
+        w1_scales = tile("w1_scales", [P, N], U8)
+        nc.vector.quantize_mx(out=w1_words[:].bitcast(FP8X4), scales=w1_scales[:], in_=w1_grouped[:])
+        w2_words = tile("w2_words", [P, N], U32)
+        w2_scales = tile("w2_scales", [P, N], U8)
+        nc.vector.quantize_mx(out=w2_words[:].bitcast(FP8X4), scales=w2_scales[:], in_=w2_grouped[:])
 
-        z_codes = tile("z_codes", [P, S], U32)
+        z_words = tile("z_words", [P, S], U32)
         z_scales = tile("z_scales", [P, S], U8)
-
-        def exp_half_h(m, cols, weights, number):
-            rows = slice(m % EARLY_TILES * P, (m % EARLY_TILES + 1) * P)
-            h_bank = bank(f"h_bank{m}_{cols.start}", cols.stop - cols.start, number)
-            moving = {2: (x2_codes, x2_scales), 1: (z_codes, z_scales)}
-            for n in (2, 1):
-                nc.tensor.matmul_mx(
-                    out=h_bank[:],
-                    lhsT=weights[n][0][:, rows].bitcast(FP8X4),
-                    lhsT_scale=weights[n][1][:, rows],
-                    rhs=moving[n][0][:, cols].bitcast(FP8X4),
-                    rhs_scale=moving[n][1][:, cols],
-                    start=(n == 2),
-                    stop=(n == 1),
-                )
-            return lambda: nc.scalar.activation(out=ex[m][:, cols], in_=h_bank[:], func=ACT.Exp, scale=0.5)
-
-        early_weights = quantize_weights(0)
-        exps = []
-        for h in range(2):
-            cols = slice(h * HALF, (h + 1) * HALF)
-            z_planes = tile(f"z_planes{h}", [P, PACK, HALF], BF16)
+        h_banks = []
+        for half in range(2):
+            cols = slice(half * HALF, (half + 1) * HALF)
+            z_planes = tile(f"z_planes{half}", [P, PACK, HALF], BF16)
+            run = P if half == 1 else HALF
             for t in range(PACK):
-                if h == 0 and t not in S_TILES_COPIED_BY_VECTOR:
-                    nc.scalar.activation(out=s_rows[t][:], in_=s_banks[t][:], func=ACT.Copy, scale=0.0625)
-                s_n1 = tile(f"s_n1_{h}{t}", [P, HALF], F32)
+                if half == 0 and t != LAST:
+                    nc.scalar.activation(out=s_rows[t][:], in_=s_banks[t][:], func=ACT.Copy, scale=S_SCALE)
+                s_n1 = tile(f"s_n1_{half}{t}", [P, HALF], F32)
                 nc.scalar.activation(
                     out=s_n1[:], in_=s_rows[t][:].indirect(entries(n1_l, cols.start, HALF)), func=ACT.Copy
                 )
-                gate = tile(f"gate{h}{t}", [P, HALF], F32)
+                gate = tile(f"gate{half}{t}", [P, HALF], F32)
                 nc.scalar.activation(
                     out=gate[:], in_=s_rows[t][:].indirect(entries(n2_l, cols.start, HALF)), func=ACT.Sigmoid
                 )
-                diff = tile(f"diff{h}{t}", [P, HALF], F32)
+                diff = tile(f"diff{half}{t}", [P, HALF], F32)
                 nc.vector.tensor_tensor(out=diff[:], in0=s_rows[t][:, cols], in1=s_n1[:], op=ALU.subtract)
-                nc.vector.scalar_tensor_tensor(
-                    out=z_planes[:, t, :], in0=diff[:], scalar=gn_sb[:, t : t + 1], in1=gate[:],
-                    op0=ALU.mult, op1=ALU.mult,
-                )
-            z_grouped = interleave(f"z_grouped{h}", z_planes)
-            nc.vector.quantize_mx(out=z_codes[:, cols].bitcast(FP8X4), scales=z_scales[:, cols], in_=z_grouped[:])
-            for m in range(EARLY_TILES):
-                exps.append(exp_half_h(m, cols, early_weights, (4 + EARLY_TILES * h + m) % 8))
+                width = run if t == LAST else HALF
+                for c in range(0, HALF, width):
+                    nc.vector.scalar_tensor_tensor(
+                        out=z_planes[:, t, c : c + width],
+                        in0=diff[:, c : c + width],
+                        scalar=gn_sb[:, t : t + 1],
+                        in1=gate[:, c : c + width],
+                        op0=ALU.mult,
+                        op1=ALU.mult,
+                    )
+            z_grouped = {c: interleave(f"z_grouped{half}_{c}", z_planes[:, :, c : c + run]) for c in range(0, HALF, run)}
+            for c in range(0, HALF, run):
+                made = slice(cols.start + c, cols.start + c + run)
+                nc.vector.quantize_mx(out=z_words[:, made].bitcast(FP8X4), scales=z_scales[:, made], in_=z_grouped[c][:])
+            for m in range(PACK):
+                rows = slice(m * P, (m + 1) * P)
+                h_bank = bank(f"h_bank{half}{m}", HALF, PACK * (1 - half) + m)
+                mx_pass(h_bank[:], (w2_words[:, rows], w2_scales[:, rows]), (x2_words[:, cols], x2_scales[:, cols]), True, False)
+                mx_pass(h_bank[:], (w1_words[:, rows], w1_scales[:, rows]), (z_words[:, cols], z_scales[:, cols]), False, True)
+                h_banks.append((h_bank, m, cols))
 
-        for run in exps:
-            run()
+        for h_bank, m, cols in h_banks:
+            nc.scalar.activation(out=ex[m][:, cols], in_=h_bank[:], func=ACT.Exp, scale=0.5)
 
-        ex_n3, ex_n4 = {}, {}
+        pieces = [(m, sum(widths[:i]), width) for m, widths in enumerate(PIECE_WIDTHS) for i, width in enumerate(widths)]
+        terms = {}
 
         def fetch_n3(u):
-            m, first, width = PIECES[u]
-            ex_n3[u] = tile(f"ex_n3_{u}", [P, width], F32, tag=f"ex_n3_{u % 2}")
-            nc.scalar.activation(out=ex_n3[u][:], in_=ex[m][:].indirect(entries(n3_l, first, width)), func=ACT.Copy)
+            m, first, width = pieces[u]
+            ex_n3 = tile(f"ex_n3_{u}", [P, width], F32, tag=f"ex_n3_{u % PIECES_AHEAD}")
+            nc.scalar.activation(out=ex_n3[:], in_=ex[m][:].indirect(entries(n3_l, first, width)), func=ACT.Copy)
+            terms[u] = [ex_n3[:]]
 
         def fetch_n4(u):
-            m, first, width = PIECES[u]
-            ex_n4[u] = tile(f"ex_n4_{u}", [P, width], F32)
+            m, first, width = pieces[u]
+            own = ex[m][:, first : first + width]
+            ex_n4 = tile(f"ex_n4_{u}", [P, width], F32)
             for c in range(0, width, HALF):
                 count = min(HALF, width - c)
                 nc.vector.tensor_copy(
-                    out=ex_n4[u][:, c : c + count], in_=ex[m][:].indirect(entries(n4_l, first + c, count))
+                    out=ex_n4[:, c : c + count], in_=ex[m][:].indirect(entries(n4_l, first + c, count))
                 )
+            if m == LAST:
+                both = tile(f"both{u}", [P, width], F32)
+                nc.vector.tensor_tensor(out=both[:], in0=ex_n4[:], in1=own, op=ALU.add)
+                terms[u] = [both[:]] + terms[u]
+            else:
+                terms[u] = [ex_n4[:], own] + terms[u]
 
-        def finish(u):
-            m, first, width = PIECES[u]
+        def divide(u):
+            m, first, width = pieces[u]
             cols = slice(first, first + width)
-            den_t = bank(f"den_t{u}", width, 4 + u % 4)
-            terms = (ex_n4[u][:], ex[m][:, cols], ex_n3[u][:])
-            for i, term in enumerate(terms):
+            den_t = bank(f"den_t{u}", width, PACK + u % PACK)
+            for i, term in enumerate(terms[u]):
                 for c in range(0, width, P):
                     nc.tensor.matmul(
-                        out=den_t[:, c : c + P], lhsT=term[:, c : c + P], rhs=ident[:], is_transpose=True,
-                        start=(i == 0 and c == 0), stop=(i == len(terms) - 1 and c + P == width),
+                        out=den_t[:, c : c + P],
+                        lhsT=term[:, c : c + P],
+                        rhs=ident[:],
+                        is_transpose=True,
+                        start=(i == 0 and c == 0),
+                        stop=(i == len(terms[u]) - 1 and c + P == width),
                     )
             root_t = tile(f"root_t{u}", [P, width], F32)
             nc.scalar.activation(out=root_t[:], in_=den_t[:], func=ACT.Abs_reciprocal_sqrt)
-            if u in SQUARED_ON_SCALAR:
-                inv_t = tile(f"inv_t{u}", [P, width], F32)
-                nc.scalar.activation(out=inv_t[:], in_=root_t[:], func=ACT.Square)
-                root_t = inv_t
-            root = bank(f"root{u}", width, u % 4)
+            root = bank(f"root{u}", width, u % PACK)
             for c in range(0, width, P):
                 nc.tensor.transpose(out=root[:, c : c + P], in_=root_t[:, c : c + P], identity=ident[:])
-            part = tile(f"part{u}", [P, width], F32)
+            partial = tile(f"partial{u}", [P, width], F32)
             nc.vector.scalar_tensor_tensor(
-                out=part[:], in0=ex[m][:, cols], scalar=2.0, in1=root[:], op0=ALU.mult, op1=ALU.mult
+                out=partial[:], in0=ex[m][:, cols], scalar=2.0, in1=root[:], op0=ALU.mult, op1=ALU.mult
             )
-            res = part
-            if u not in SQUARED_ON_SCALAR:
-                res = tile(f"res{u}", [P, width], F32)
-                nc.vector.tensor_tensor(out=res[:], in0=part[:], in1=root[:], op=ALU.mult)
-            nc.sync.dma_start(out=out[m * P : (m + 1) * P, cols], in_=res[:])
+            share = tile(f"share{u}", [P, width], F32)
+            nc.vector.tensor_tensor(out=share[:], in0=partial[:], in1=root[:], op=ALU.mult)
+            nc.sync.dma_start(out=out[m * P : (m + 1) * P, cols], in_=share[:])
 
-        for u in range(2):
+        for u in range(PIECES_AHEAD):
             fetch_n3(u)
-        for u in range(2, 2):
-            fetch_n3(u)
-        for u in range(2):
+        for u in range(PIECES_AHEAD):
             fetch_n4(u)
-        for u in range(len(PIECES)):
-            finish(u)
-            if u + 2 < len(PIECES):
-                fetch_n3(u + 2)
-            if u + 2 < len(PIECES):
-                fetch_n4(u + 2)
+        for u in range(len(pieces)):
+            divide(u)
+            if u + PIECES_AHEAD < len(pieces):
+                fetch_n3(u + PIECES_AHEAD)
+                fetch_n4(u + PIECES_AHEAD)

from contextlib import ExitStack

import concourse.mybir as mybir
from concourse.masks import make_identity

K, T, S, N, G, H = 512, 2048, 512, 512, 2048, 512
FLOPS = 2 * K * H * S + 2 * H * N * S + 2 * K * N * S

F32 = mybir.dt.float32
BF16 = mybir.dt.bfloat16
I32 = mybir.dt.int32
U32 = mybir.dt.uint32
U16 = mybir.dt.uint16
U8 = mybir.dt.uint8
FP8X4 = mybir.dt.float8_e4m3fn_x4
ACT = mybir.ActivationFunctionType
ALU = mybir.AluOpType

P = 128
PACK = 4
LAST = PACK - 1
HALF = S // 2
S_SCALE = 0.0625
LIST_GROUP = 16
BLOCK_PARTITIONS = 8
QUADRANT = 32
SPARE = 32
PIECE_WIDTHS = ((S,), (S,), (HALF, HALF), (HALF, P, P))
PIECES_AHEAD = 2


def tile_picked_kmixgdifshare_none_p_kernel(
    tc, x_words, x_scales, d_words, d_scales, gn, w1, w2, offs, k1, n1, n2, two, n3, n4, out
):
    nc = tc.nc
    with ExitStack() as ctx:
        sb = ctx.enter_context(tc.tile_pool(name="sb", bufs=1))
        ps = ctx.enter_context(tc.psum_pool(name="ps", bufs=1))

        def tile(name, shape, dtype, tag=None):
            return sb.tile(shape, dtype, name=name, tag=tag or name, align_bytes=64)

        def bank(name, width, number):
            return ps.tile([P, width], F32, name=name, tag=f"bank{number}")

        def load_list(name, src):
            lst = sb.tile([P, S // LIST_GROUP], U16, name=name)
            nc.sync.dma_start(lst[:], src)
            return lst

        def entries(lst, first, count):
            return lst[:, first // LIST_GROUP : (first + count) // LIST_GROUP]

        def mx_pass(acc, stationary, moving, start, stop):
            nc.tensor.matmul_mx(
                out=acc,
                lhsT=stationary[0].bitcast(FP8X4),
                lhsT_scale=stationary[1],
                rhs=moving[0].bitcast(FP8X4),
                rhs_scale=moving[1],
                start=start,
                stop=stop,
            )

        d_scale_win = tile("d_scale_win", [P, G], U8)
        x_scale_win = tile("x_scale_win", [P, T], U8)
        nc.vector.memset(d_scale_win[:].bitcast(I32), 0)
        nc.vector.memset(x_scale_win[:].bitcast(I32), 0)

        warm_in = tile("warm_in", [P, 1], F32)
        nc.gpsimd.memset(warm_in[:], 0.0)
        warm_out = tile("warm_out", [P, 1], F32)
        nc.scalar.activation(out=warm_out[:], in_=warm_in[:], func=ACT.Sigmoid)

        k1_l = load_list("k1_l", k1)
        offs_l = load_list("offs_l", offs)
        nc.sync.dma_start(out=d_scale_win[0:P:BLOCK_PARTITIONS, :].bitcast(I32), in_=d_scales[0].bitcast(I32))
        d_word_win = tile("d_word_win", [P, G], I32)
        nc.sync.dma_start(out=d_word_win[:], in_=d_words[0].rearrange("p c r -> p (c r)").bitcast(I32))
        for q in range(P // QUADRANT):
            queue = nc.sync if q == 0 else nc.scalar
            queue.dma_start(
                out=x_scale_win[QUADRANT * q : QUADRANT * q + 4, :].bitcast(I32),
                in_=x_scales[0][4 * q : 4 * q + 4, :].bitcast(I32),
            )
        n1_l = load_list("n1_l", n1)
        x_word_win = tile("x_word_win", [P, T], I32)
        nc.sync.dma_start(out=x_word_win[:], in_=x_words[0].rearrange("p c r -> p (c r)").bitcast(I32))
        n2_l = load_list("n2_l", n2)
        two_l = load_list("two_l", two)
        n3_l = load_list("n3_l", n3)
        n4_l = load_list("n4_l", n4)
        gn_sb = tile("gn_sb", [P, PACK], F32)
        nc.gpsimd.dma_start(out=gn_sb[:], in_=gn.rearrange("(p t) o -> p (t o)", t=PACK))
        ident = tile("ident", [P, P], F32)
        make_identity(nc, ident[:])
        ex = []
        for m, widths in enumerate(PIECE_WIDTHS):
            spare = SPARE if S in widths else 0
            ex.append(tile(f"ex{m}", [P, S + spare], F32))
            if spare:
                nc.gpsimd.memset(ex[m][:, S:], 0.0)

        key_bytes = tile("key_bytes", [P, H], U8)
        nc.vector.tensor_copy(out=key_bytes[:], in_=d_scale_win[:].indirect(k1_l[:]))
        key_bytes_dealt = tile("key_bytes_dealt", [P, H], U8)
        nc.vector.tensor_copy(
            out=key_bytes_dealt[:].rearrange("p (t c i) -> p c t i", t=PACK, i=16),
            in_=key_bytes[:].rearrange("p (c i t) -> p c t i", t=PACK, i=16),
        )
        key_scales = tile("key_scales", [P, H], U8)
        nc.vector.tensor_copy(out=key_scales[:].bitcast(I32), in_=key_bytes_dealt[:].bitcast(I32))
        for r in range(1, 4):
            nc.scalar.dma_start(
                out=key_scales[r:P:QUADRANT, :].bitcast(I32),
                in_=key_bytes_dealt[BLOCK_PARTITIONS * r : P : QUADRANT, :].bitcast(I32),
            )
        xq_scales = tile("xq_scales", [P, S], U8)
        nc.vector.tensor_copy(out=xq_scales[:], in_=x_scale_win[:].indirect(offs_l[:]))
        key_words = tile("key_words", [P, H], U32)
        nc.vector.tensor_copy(out=key_words[:], in_=d_word_win[:].bitcast(U32).indirect(k1_l[:]))
        key_words_dealt = tile("key_words_dealt", [P, H], U32)
        nc.vector.tensor_copy(
            out=key_words_dealt[:].rearrange("p (t c i) -> p c t i", t=PACK, i=4),
            in_=key_words[:].rearrange("p (c i t) -> p c t i", t=PACK, i=4),
        )

        w1_raw = tile("w1_raw", [P, PACK, N], F32, tag="d_word_win")
        nc.sync.dma_start(out=w1_raw[:], in_=w1.rearrange("(p t) m -> p t m", t=PACK))
        w2_raw = tile("w2_raw", [P, PACK, N], F32, tag="key_words")
        nc.sync.dma_start(out=w2_raw[:], in_=w2.rearrange("(p t) m -> p t m", t=PACK))
        xq_words = tile("xq_words", [P, S], U32)
        nc.vector.tensor_copy(out=xq_words[:], in_=x_word_win[:].bitcast(U32).indirect(offs_l[:]))

        s_banks = [bank(f"s_bank{t}", S, t) for t in range(PACK)]
        for t in range(PACK):
            keys = slice(t * P, (t + 1) * P)
            mx_pass(s_banks[t][:], (key_words_dealt[:, keys], key_scales[:, keys]), (xq_words[:], xq_scales[:]), True, True)
        s_rows = [tile(f"s_rows{t}", [P, S], F32) for t in range(PACK)]
        nc.vector.tensor_scalar_mul(out=s_rows[LAST][:], in0=s_banks[LAST][:], scalar1=S_SCALE)

        x2_words = tile("x2_words", [P, S], U32)
        nc.vector.tensor_copy(out=x2_words[:], in_=x_word_win[:].bitcast(U32).indirect(two_l[:]))
        x2_scales = tile("x2_scales", [P, S], U8)
        nc.vector.tensor_copy(out=x2_scales[:], in_=x_scale_win[:].indirect(two_l[:]))

        def interleave(name, planes):
            grouped = tile(name, [P, planes.shape[2] * PACK], BF16)
            nc.vector.tensor_copy(
                out=grouped[:].rearrange("p (c i t) -> p c t i", t=PACK, i=4),
                in_=planes.rearrange("p t (c i) -> p c t i", i=4),
            )
            return grouped

        w1_grouped = interleave("w1_grouped", w1_raw[:])
        w2_grouped = interleave("w2_grouped", w2_raw[:])
        w1_words = tile("w1_words", [P, N], U32)
        w1_scales = tile("w1_scales", [P, N], U8)
        nc.vector.quantize_mx(out=w1_words[:].bitcast(FP8X4), scales=w1_scales[:], in_=w1_grouped[:])
        w2_words = tile("w2_words", [P, N], U32)
        w2_scales = tile("w2_scales", [P, N], U8)
        nc.vector.quantize_mx(out=w2_words[:].bitcast(FP8X4), scales=w2_scales[:], in_=w2_grouped[:])

        z_words = tile("z_words", [P, S], U32)
        z_scales = tile("z_scales", [P, S], U8)
        h_banks = []
        for half in range(2):
            cols = slice(half * HALF, (half + 1) * HALF)
            z_planes = tile(f"z_planes{half}", [P, PACK, HALF], BF16)
            run = P if half == 1 else HALF
            for t in range(PACK):
                if half == 0 and t != LAST:
                    nc.scalar.activation(out=s_rows[t][:], in_=s_banks[t][:], func=ACT.Copy, scale=S_SCALE)
                s_n1 = tile(f"s_n1_{half}{t}", [P, HALF], F32)
                nc.scalar.activation(
                    out=s_n1[:], in_=s_rows[t][:].indirect(entries(n1_l, cols.start, HALF)), func=ACT.Copy
                )
                gate = tile(f"gate{half}{t}", [P, HALF], F32)
                nc.scalar.activation(
                    out=gate[:], in_=s_rows[t][:].indirect(entries(n2_l, cols.start, HALF)), func=ACT.Sigmoid
                )
                diff = tile(f"diff{half}{t}", [P, HALF], F32)
                nc.vector.tensor_tensor(out=diff[:], in0=s_rows[t][:, cols], in1=s_n1[:], op=ALU.subtract)
                width = run if t == LAST else HALF
                for c in range(0, HALF, width):
                    nc.vector.scalar_tensor_tensor(
                        out=z_planes[:, t, c : c + width],
                        in0=diff[:, c : c + width],
                        scalar=gn_sb[:, t : t + 1],
                        in1=gate[:, c : c + width],
                        op0=ALU.mult,
                        op1=ALU.mult,
                    )
            z_grouped = {c: interleave(f"z_grouped{half}_{c}", z_planes[:, :, c : c + run]) for c in range(0, HALF, run)}
            for c in range(0, HALF, run):
                made = slice(cols.start + c, cols.start + c + run)
                nc.vector.quantize_mx(out=z_words[:, made].bitcast(FP8X4), scales=z_scales[:, made], in_=z_grouped[c][:])
            for m in range(PACK):
                rows = slice(m * P, (m + 1) * P)
                h_bank = bank(f"h_bank{half}{m}", HALF, PACK * (1 - half) + m)
                mx_pass(h_bank[:], (w2_words[:, rows], w2_scales[:, rows]), (x2_words[:, cols], x2_scales[:, cols]), True, False)
                mx_pass(h_bank[:], (w1_words[:, rows], w1_scales[:, rows]), (z_words[:, cols], z_scales[:, cols]), False, True)
                h_banks.append((h_bank, m, cols))

        for h_bank, m, cols in h_banks:
            nc.scalar.activation(out=ex[m][:, cols], in_=h_bank[:], func=ACT.Exp, scale=0.5)

        pieces = [(m, sum(widths[:i]), width) for m, widths in enumerate(PIECE_WIDTHS) for i, width in enumerate(widths)]
        terms = {}

        def fetch_n3(u):
            m, first, width = pieces[u]
            ex_n3 = tile(f"ex_n3_{u}", [P, width], F32, tag=f"ex_n3_{u % PIECES_AHEAD}")
            nc.scalar.activation(out=ex_n3[:], in_=ex[m][:].indirect(entries(n3_l, first, width)), func=ACT.Copy)
            terms[u] = [ex_n3[:]]

        def fetch_n4(u):
            m, first, width = pieces[u]
            own = ex[m][:, first : first + width]
            ex_n4 = tile(f"ex_n4_{u}", [P, width], F32)
            for c in range(0, width, HALF):
                count = min(HALF, width - c)
                nc.vector.tensor_copy(
                    out=ex_n4[:, c : c + count], in_=ex[m][:].indirect(entries(n4_l, first + c, count))
                )
            if m == LAST:
                both = tile(f"both{u}", [P, width], F32)
                nc.vector.tensor_tensor(out=both[:], in0=ex_n4[:], in1=own, op=ALU.add)
                terms[u] = [both[:]] + terms[u]
            else:
                terms[u] = [ex_n4[:], own] + terms[u]

        def divide(u):
            m, first, width = pieces[u]
            cols = slice(first, first + width)
            den_t = bank(f"den_t{u}", width, PACK + u % PACK)
            for i, term in enumerate(terms[u]):
                for c in range(0, width, P):
                    nc.tensor.matmul(
                        out=den_t[:, c : c + P],
                        lhsT=term[:, c : c + P],
                        rhs=ident[:],
                        is_transpose=True,
                        start=(i == 0 and c == 0),
                        stop=(i == len(terms[u]) - 1 and c + P == width),
                    )
            root_t = tile(f"root_t{u}", [P, width], F32)
            nc.scalar.activation(out=root_t[:], in_=den_t[:], func=ACT.Abs_reciprocal_sqrt)
            root = bank(f"root{u}", width, u % PACK)
            for c in range(0, width, P):
                nc.tensor.transpose(out=root[:, c : c + P], in_=root_t[:, c : c + P], identity=ident[:])
            partial = tile(f"partial{u}", [P, width], F32)
            nc.vector.scalar_tensor_tensor(
                out=partial[:], in0=ex[m][:, cols], scalar=2.0, in1=root[:], op0=ALU.mult, op1=ALU.mult
            )
            share = tile(f"share{u}", [P, width], F32)
            nc.vector.tensor_tensor(out=share[:], in0=partial[:], in1=root[:], op=ALU.mult)
            nc.sync.dma_start(out=out[m * P : (m + 1) * P, cols], in_=share[:])

        for u in range(PIECES_AHEAD):
            fetch_n3(u)
        for u in range(PIECES_AHEAD):
            fetch_n4(u)
        for u in range(len(pieces)):
            divide(u)
            if u + PIECES_AHEAD < len(pieces):
                fetch_n3(u + PIECES_AHEAD)
                fetch_n4(u + PIECES_AHEAD)
